import numpy as np
import ml_dtypes


def mxq(x, axis, fmt="e4m3"):
    dtype, down = {"e4m3": (ml_dtypes.float8_e4m3fn, 7), "e5m2": (ml_dtypes.float8_e5m2, 14)}[fmt]
    v = np.moveaxis(np.asarray(x, np.float32).astype(ml_dtypes.bfloat16).astype(np.float64), axis, -1)
    blocks = v.reshape(v.shape[:-1] + (-1, 32))
    amax = np.abs(blocks).max(-1, keepdims=True)
    byte = np.maximum(np.where(amax > 0, np.frexp(amax)[1] - 1 + 127, 0) - down, 1)
    scale = np.exp2(byte - 127.0)
    codes = (blocks / scale).astype(np.float32).astype(dtype).astype(np.float64)
    return np.moveaxis((codes * scale).reshape(v.shape), -1, axis)


WIDE = False


def mx_kscale(k):
    if not WIDE:
        return np.ones(k)
    levels = np.array([10, -10, 5, -5, 0])
    if k % 512:
        return np.exp2(np.random.permutation(np.resize(levels, k // 32))).repeat(32)
    a = np.empty((k // 512, 16))
    for p in range(k // 512):
        a[p, :8] = np.random.permutation(np.resize(levels, 8))
        for g in range(8):
            far = levels[np.abs(levels - a[p, g]) >= 10]
            a[p, g + 8] = far[np.random.randint(len(far))]
    return np.exp2(a.ravel()).repeat(32)


def f64(x):
    return np.asarray(x).astype(np.float64)


def striped(idx):
    return np.tile(idx.reshape(-1, 16).T, (8, 1)).astype(np.uint16)


def unstriped(offs):
    return offs[:16].T.reshape(-1).astype(np.int64)


def pack_weight(w):
    k, n = w.shape
    w = f64(np.asarray(w, np.float32).astype(ml_dtypes.bfloat16)).reshape(k // 32, 32, n)
    amax = np.abs(w).max(1)
    byte = np.clip(np.where(amax > 0, np.frexp(amax)[1] - 1 + 127 - 7, 1), 1, 254)
    scaled = (w * np.exp2(127.0 - byte)[:, None, :]).reshape(k, n).astype(np.float32)
    words = np.ascontiguousarray(scaled.reshape(k // 512, 128, 4, n).transpose(0, 1, 3, 2)).astype(ml_dtypes.float8_e4m3fn).view(np.uint8)
    return words, np.ascontiguousarray(byte.astype(np.uint8).reshape(k // 512, 16, n))


def unpack_weight(words, scales):
    g, p, n, _ = words.shape
    vals = np.ascontiguousarray(words).view(ml_dtypes.float8_e4m3fn).astype(np.float64) * np.repeat(np.exp2(scales.astype(np.float64) - 127.0), 8, axis=1)[..., None]
    return vals.transpose(0, 1, 3, 2).reshape(g * 512, n)


K, T, S, D, N = 512, 2048, 512, 2, 256


def setup_inputs():
    n = np.random.standard_normal
    s = mx_kscale(K)[:, None]
    packed_xT = pack_weight(n((K, T)) * s)
    return {
        "x_words": packed_xT[0],
        "x_scales": packed_xT[1],
        "w1": (n((K, N)) / np.sqrt(K) / s).astype(np.float32),
        "w2": (n((K, N)) / np.sqrt(K) / s).astype(np.float32),
        "offs": striped(np.random.permutation(T)[:S]),
    }


def reference(x_words, x_scales, w1, w2, offs):
    xq = unpack_weight(x_words, x_scales)[:, unstriped(offs)]
    z = mxq(f64(w2), 0, "e4m3").T @ xq
    phi = (z) ** 2
    y = mxq(f64(w1), 0, "e4m3").T @ xq
    rho = np.exp(0.5 * y)
    dens = rho.reshape(len(rho), -1, D).sum(axis=2) + 0.5
    return 0.5 * (phi.reshape(len(phi), -1, D).sum(axis=2)) - (1.5 * np.sqrt(dens))

@@ -1,0 +1,130 @@
+from contextlib import ExitStack
+
+import concourse.mybir as mybir
+
+K, T, S, D, N = 512, 2048, 512, 2, 256
+FLOPS = 2 * 2 * K * N * S
+
+F32 = mybir.dt.float32
+BF16 = mybir.dt.bfloat16
+I32 = mybir.dt.int32
+U32 = mybir.dt.uint32
+U16 = mybir.dt.uint16
+U8 = mybir.dt.uint8
+FP8X4 = mybir.dt.float8_e4m3fn_x4
+ACT = mybir.ActivationFunctionType
+ALU = mybir.AluOpType
+
+P = 128
+PACK = 4
+HALF = S // 2
+ATOMS = HALF // D
+LIST_COLS = HALF // 16
+
+
+def tile_picked_yeamf_en_p_kernel(tc, x_words, x_scales, w1, w2, offs, out):
+    nc = tc.nc
+    with ExitStack() as ctx:
+        sb = ctx.enter_context(tc.tile_pool(name="sb", bufs=1))
+        ps = ctx.enter_context(tc.psum_pool(name="ps", bufs=1))
+
+        offsets = sb.tile([P, S // 16], U16, name="offsets")
+        nc.sync.dma_start(offsets[:], offs)
+
+        store_scales = sb.tile([P, T], U8, name="store_scales", align_bytes=64)
+        nc.vector.memset(store_scales[:].bitcast(I32), 0)
+        for q in range(4):
+            nc.scalar.dma_start(
+                store_scales[32 * q : 32 * q + 4, :].bitcast(I32),
+                x_scales[0, 4 * q : 4 * q + 4, :].bitcast(I32),
+            )
+
+        w1_raw = sb.tile([P, PACK, N], F32, name="w1_raw")
+        nc.sync.dma_start(w1_raw[:], w1.rearrange("(p j) m -> p j m", j=PACK))
+        store_words = sb.tile([P, T], I32, name="store_words", align_bytes=64)
+        nc.sync.dma_start(store_words[:], x_words[0].rearrange("p n t -> p (n t)").bitcast(I32))
+        w2_raw = sb.tile([P, PACK, N], F32, name="w2_raw")
+        nc.sync.dma_start(w2_raw[:], w2.rearrange("(p j) m -> p j m", j=PACK))
+
+        def interleave_views(grouped, raw):
+            return (
+                grouped.rearrange("p (c i) j -> p c j i", i=4),
+                raw.rearrange("p j (c i) -> p c j i", i=4),
+            )
+
+        w1_grouped = sb.tile([P, N, PACK], BF16, name="w1_grouped", align_bytes=64)
+        dst, src = interleave_views(w1_grouped[:], w1_raw[:])
+        nc.scalar.activation(dst, src, ACT.Copy)
+        picked_scales = sb.tile([P, S], U8, name="picked_scales", align_bytes=64)
+        nc.vector.tensor_copy(picked_scales[:], store_scales[:].indirect(offsets[:]))
+        w1_codes = sb.tile([P, N], U32, name="w1_codes", align_bytes=64)
+        w1_scales = sb.tile([P, N], U8, name="w1_scales", align_bytes=64)
+        nc.vector.quantize_mx(
+            out=w1_codes[:].bitcast(FP8X4), scales=w1_scales[:], in_=w1_grouped[:].rearrange("p m j -> p (m j)")
+        )
+
+        picked_words = [sb.tile([P, HALF], U32, name=f"picked_words{h}", align_bytes=64) for h in range(2)]
+
+        def product(codes, scales, mt, h, name):
+            bank = ps.tile([P, 512], F32, name=name)
+            nc.tensor.matmul_mx(
+                out=bank[:, :HALF],
+                lhsT=codes.bitcast(FP8X4),
+                lhsT_scale=scales,
+                rhs=picked_words[h][:].bitcast(FP8X4),
+                rhs_scale=picked_scales[:, h * HALF : (h + 1) * HALF],
+                start=True,
+                stop=True,
+            )
+            return bank[:, :HALF].rearrange("p (v d) -> p d v", d=D)
+
+        rho = [sb.tile([P, D, N], F32, name=f"rho{mt}") for mt in range(2)]
+        for h in range(2):
+            nc.vector.tensor_copy(
+                picked_words[h][:],
+                store_words[:].bitcast(U32).indirect(offsets[:, h * LIST_COLS : (h + 1) * LIST_COLS]),
+            )
+            for mt in range(2):
+                cols = slice(mt * P, (mt + 1) * P)
+                y = product(w1_codes[:, cols], w1_scales[:, cols], mt, h, f"y{mt}{h}")
+                nc.scalar.activation(rho[mt][:, :, h * ATOMS : (h + 1) * ATOMS], y, ACT.Exp, scale=0.5)
+
+        w2_grouped = [sb.tile([P, P, PACK], BF16, name=f"w2_grouped{mt}", align_bytes=64) for mt in range(2)]
+        w2_codes = [sb.tile([P, P], U32, name=f"w2_codes{mt}", align_bytes=64) for mt in range(2)]
+        w2_scales = [sb.tile([P, P], U8, name=f"w2_scales{mt}", align_bytes=64) for mt in range(2)]
+        for mt in range(2):
+            dst, src = interleave_views(w2_grouped[mt][:], w2_raw[:, :, mt * P : (mt + 1) * P])
+            nc.vector.tensor_copy(dst, src)
+        for mt in range(2):
+            nc.vector.quantize_mx(
+                out=w2_codes[mt][:].bitcast(FP8X4),
+                scales=w2_scales[mt][:],
+                in_=w2_grouped[mt][:].rearrange("p m j -> p (m j)"),
+            )
+        z = [[product(w2_codes[mt][:], w2_scales[mt][:], mt, h, f"z{mt}{h}") for h in range(2)] for mt in range(2)]
+
+        dens = [sb.tile([P, N], F32, name=f"dens{mt}") for mt in range(2)]
+        for mt in range(2):
+            nc.vector.tensor_tensor(dens[mt][:], rho[mt][:, 0, :], rho[mt][:, 1, :], ALU.add)
+
+        phi = [sb.tile([P, D, N], F32, name=f"phi{mt}") for mt in range(2)]
+        z_copy = sb.tile([P, D, N], F32, name="z_copy")
+        embed = [sb.tile([P, N], F32, name=f"embed{mt}") for mt in range(2)]
+        pair = [sb.tile([P, N], F32, name=f"pair{mt}") for mt in range(2)]
+        energy = [sb.tile([P, N], F32, name=f"energy{mt}") for mt in range(2)]
+
+        for h in range(2):
+            nc.vector.tensor_copy(z_copy[:, :, h * ATOMS : (h + 1) * ATOMS], z[0][h])
+        for h in range(2):
+            atoms = slice(h * ATOMS, (h + 1) * ATOMS)
+            nc.vector.tensor_tensor(phi[0][:, :, atoms], z[0][h], z_copy[:, :, atoms], ALU.mult)
+
+        nc.scalar.activation(embed[0][:], dens[0][:], ACT.Sqrt, scale=2.25, bias=1.125)
+        for h in range(2):
+            nc.scalar.activation(phi[1][:, :, h * ATOMS : (h + 1) * ATOMS], z[1][h], ACT.Square)
+        nc.scalar.activation(embed[1][:], dens[1][:], ACT.Sqrt, scale=2.25, bias=1.125)
+
+        for mt in range(2):
+            nc.vector.tensor_tensor(pair[mt][:], phi[mt][:, 0, :], phi[mt][:, 1, :], ALU.add)
+            nc.vector.scalar_tensor_tensor(energy[mt][:], pair[mt][:], 0.5, embed[mt][:], ALU.mult, ALU.subtract)
+            nc.sync.dma_start(out[mt * P : (mt + 1) * P, :], energy[mt][:])

@@ -33,15 +33,14 @@ def tile_picked_yeamf_en_p_kernel(tc, x_words, x_scales, w1, w2, offs, out):
 
         store_scales = sb.tile([P, T], U8, name="store_scales", align_bytes=64)
         nc.vector.memset(store_scales[:].bitcast(I32), 0)
+        w1_raw = sb.tile([P, PACK, N], F32, name="w1_raw")
+        nc.sync.dma_start(w1_raw[:], w1.rearrange("(p j) m -> p j m", j=PACK))
         for q in range(4):
-            nc.scalar.dma_start(
+            nc.sync.dma_start(
                 store_scales[32 * q : 32 * q + 4, :].bitcast(I32),
                 x_scales[0, 4 * q : 4 * q + 4, :].bitcast(I32),
             )
-
-        w1_raw = sb.tile([P, PACK, N], F32, name="w1_raw")
-        nc.sync.dma_start(w1_raw[:], w1.rearrange("(p j) m -> p j m", j=PACK))
-        store_words = sb.tile([P, T], I32, name="store_words", align_bytes=64)
+        store_words = sb.tile([P, T], I32, name="store_words", tag="words_then_w2", align_bytes=64)
         nc.sync.dma_start(store_words[:], x_words[0].rearrange("p n t -> p (n t)").bitcast(I32))
         w2_raw = sb.tile([P, PACK, N], F32, name="w2_raw")
         nc.sync.dma_start(w2_raw[:], w2.rearrange("(p j) m -> p j m", j=PACK))
@@ -78,7 +77,7 @@ def tile_picked_yeamf_en_p_kernel(tc, x_words, x_scales, w1, w2, offs, out):
             )
             return bank[:, :HALF].rearrange("p (v d) -> p d v", d=D)
 
-        rho = [sb.tile([P, D, N], F32, name=f"rho{mt}") for mt in range(2)]
+        rho = [sb.tile([P, D, 2, ATOMS], F32, name=f"rho{h}") for h in range(2)]
         for h in range(2):
             nc.vector.tensor_copy(
                 picked_words[h][:],
@@ -87,44 +86,46 @@ def tile_picked_yeamf_en_p_kernel(tc, x_words, x_scales, w1, w2, offs, out):
             for mt in range(2):
                 cols = slice(mt * P, (mt + 1) * P)
                 y = product(w1_codes[:, cols], w1_scales[:, cols], mt, h, f"y{mt}{h}")
-                nc.scalar.activation(rho[mt][:, :, h * ATOMS : (h + 1) * ATOMS], y, ACT.Exp, scale=0.5)
+                nc.scalar.activation(rho[h][:, :, mt, :], y, ACT.Exp, scale=0.5)
 
-        w2_grouped = [sb.tile([P, P, PACK], BF16, name=f"w2_grouped{mt}", align_bytes=64) for mt in range(2)]
+        w2_grouped = sb.tile([P, N, PACK], BF16, name="w2_grouped", tag="words_then_w2", align_bytes=64)
         w2_codes = [sb.tile([P, P], U32, name=f"w2_codes{mt}", align_bytes=64) for mt in range(2)]
         w2_scales = [sb.tile([P, P], U8, name=f"w2_scales{mt}", align_bytes=64) for mt in range(2)]
         for mt in range(2):
-            dst, src = interleave_views(w2_grouped[mt][:], w2_raw[:, :, mt * P : (mt + 1) * P])
+            dst, src = interleave_views(w2_grouped[:, mt * P : (mt + 1) * P, :], w2_raw[:, :, mt * P : (mt + 1) * P])
             nc.vector.tensor_copy(dst, src)
         for mt in range(2):
             nc.vector.quantize_mx(
                 out=w2_codes[mt][:].bitcast(FP8X4),
                 scales=w2_scales[mt][:],
-                in_=w2_grouped[mt][:].rearrange("p m j -> p (m j)"),
+                in_=w2_grouped[:, mt * P : (mt + 1) * P, :].rearrange("p m j -> p (m j)"),
             )
         z = [[product(w2_codes[mt][:], w2_scales[mt][:], mt, h, f"z{mt}{h}") for h in range(2)] for mt in range(2)]
 
-        dens = [sb.tile([P, N], F32, name=f"dens{mt}") for mt in range(2)]
-        for mt in range(2):
-            nc.vector.tensor_tensor(dens[mt][:], rho[mt][:, 0, :], rho[mt][:, 1, :], ALU.add)
-
+        dens = sb.tile([P, 2, N], F32, name="dens")
         phi = [sb.tile([P, D, N], F32, name=f"phi{mt}") for mt in range(2)]
-        z_copy = sb.tile([P, D, N], F32, name="z_copy")
+        z_copy = [sb.tile([P, D, ATOMS], F32, name=f"z_copy{h}") for h in range(2)]
         embed = [sb.tile([P, N], F32, name=f"embed{mt}") for mt in range(2)]
         pair = [sb.tile([P, N], F32, name=f"pair{mt}") for mt in range(2)]
         energy = [sb.tile([P, N], F32, name=f"energy{mt}") for mt in range(2)]
 
-        for h in range(2):
-            nc.vector.tensor_copy(z_copy[:, :, h * ATOMS : (h + 1) * ATOMS], z[0][h])
-        for h in range(2):
-            atoms = slice(h * ATOMS, (h + 1) * ATOMS)
-            nc.vector.tensor_tensor(phi[0][:, :, atoms], z[0][h], z_copy[:, :, atoms], ALU.mult)
+        def atoms(h):
+            return slice(h * ATOMS, (h + 1) * ATOMS)
 
-        nc.scalar.activation(embed[0][:], dens[0][:], ACT.Sqrt, scale=2.25, bias=1.125)
-        for h in range(2):
-            nc.scalar.activation(phi[1][:, :, h * ATOMS : (h + 1) * ATOMS], z[1][h], ACT.Square)
-        nc.scalar.activation(embed[1][:], dens[1][:], ACT.Sqrt, scale=2.25, bias=1.125)
-
-        for mt in range(2):
+        def add_pairs(mt):
             nc.vector.tensor_tensor(pair[mt][:], phi[mt][:, 0, :], phi[mt][:, 1, :], ALU.add)
+
+        for h in range(2):
+            nc.scalar.activation(phi[0][:, :, atoms(h)], z[0][h], ACT.Square)
+        for h in range(2):
+            nc.vector.tensor_tensor(dens[:, :, atoms(h)], rho[h][:, 0, :, :], rho[h][:, 1, :, :], ALU.add)
+        for h in range(2):
+            nc.vector.tensor_copy(z_copy[h][:], z[1][h])
+        for h in range(2):
+            nc.vector.tensor_tensor(phi[1][:, :, atoms(h)], z[1][h], z_copy[h][:], ALU.mult)
+        for mt in range(2):
+            add_pairs(mt)
+        for mt in range(2):
+            nc.scalar.activation(embed[mt][:], dens[:, mt, :], ACT.Sqrt, scale=2.25, bias=1.125)
             nc.vector.scalar_tensor_tensor(energy[mt][:], pair[mt][:], 0.5, embed[mt][:], ALU.mult, ALU.subtract)
             nc.sync.dma_start(out[mt * P : (mt + 1) * P, :], energy[mt][:])

from contextlib import ExitStack

import concourse.mybir as mybir

K, T, S, D, N = 512, 2048, 512, 2, 256
FLOPS = 2 * 2 * K * N * S

F32 = mybir.dt.float32
BF16 = mybir.dt.bfloat16
I32 = mybir.dt.int32
U32 = mybir.dt.uint32
U16 = mybir.dt.uint16
U8 = mybir.dt.uint8
FP8X4 = mybir.dt.float8_e4m3fn_x4
ACT = mybir.ActivationFunctionType
ALU = mybir.AluOpType

P = 128
PACK = 4
HALF = S // 2
ATOMS = HALF // D
LIST_COLS = HALF // 16


def tile_picked_yeamf_en_p_kernel(tc, x_words, x_scales, w1, w2, offs, out):
    nc = tc.nc
    with ExitStack() as ctx:
        sb = ctx.enter_context(tc.tile_pool(name="sb", bufs=1))
        ps = ctx.enter_context(tc.psum_pool(name="ps", bufs=1))

        offsets = sb.tile([P, S // 16], U16, name="offsets")
        nc.sync.dma_start(offsets[:], offs)

        store_scales = sb.tile([P, T], U8, name="store_scales", align_bytes=64)
        nc.vector.memset(store_scales[:].bitcast(I32), 0)
        w1_raw = sb.tile([P, PACK, N], F32, name="w1_raw")
        nc.sync.dma_start(w1_raw[:], w1.rearrange("(p j) m -> p j m", j=PACK))
        for q in range(4):
            nc.sync.dma_start(
                store_scales[32 * q : 32 * q + 4, :].bitcast(I32),
                x_scales[0, 4 * q : 4 * q + 4, :].bitcast(I32),
            )
        store_words = sb.tile([P, T], I32, name="store_words", tag="words_then_w2", align_bytes=64)
        nc.sync.dma_start(store_words[:], x_words[0].rearrange("p n t -> p (n t)").bitcast(I32))
        w2_raw = sb.tile([P, PACK, N], F32, name="w2_raw")
        nc.sync.dma_start(w2_raw[:], w2.rearrange("(p j) m -> p j m", j=PACK))

        def interleave_views(grouped, raw):
            return (
                grouped.rearrange("p (c i) j -> p c j i", i=4),
                raw.rearrange("p j (c i) -> p c j i", i=4),
            )

        w1_grouped = sb.tile([P, N, PACK], BF16, name="w1_grouped", align_bytes=64)
        dst, src = interleave_views(w1_grouped[:], w1_raw[:])
        nc.scalar.activation(dst, src, ACT.Copy)
        picked_scales = sb.tile([P, S], U8, name="picked_scales", align_bytes=64)
        nc.vector.tensor_copy(picked_scales[:], store_scales[:].indirect(offsets[:]))
        w1_codes = sb.tile([P, N], U32, name="w1_codes", align_bytes=64)
        w1_scales = sb.tile([P, N], U8, name="w1_scales", align_bytes=64)
        nc.vector.quantize_mx(
            out=w1_codes[:].bitcast(FP8X4), scales=w1_scales[:], in_=w1_grouped[:].rearrange("p m j -> p (m j)")
        )

        picked_words = [sb.tile([P, HALF], U32, name=f"picked_words{h}", align_bytes=64) for h in range(2)]

        def product(codes, scales, mt, h, name):
            bank = ps.tile([P, 512], F32, name=name)
            nc.tensor.matmul_mx(
                out=bank[:, :HALF],
                lhsT=codes.bitcast(FP8X4),
                lhsT_scale=scales,
                rhs=picked_words[h][:].bitcast(FP8X4),
                rhs_scale=picked_scales[:, h * HALF : (h + 1) * HALF],
                start=True,
                stop=True,
            )
            return bank[:, :HALF].rearrange("p (v d) -> p d v", d=D)

        rho = [sb.tile([P, D, 2, ATOMS], F32, name=f"rho{h}") for h in range(2)]
        for h in range(2):
            nc.vector.tensor_copy(
                picked_words[h][:],
                store_words[:].bitcast(U32).indirect(offsets[:, h * LIST_COLS : (h + 1) * LIST_COLS]),
            )
            for mt in range(2):
                cols = slice(mt * P, (mt + 1) * P)
                y = product(w1_codes[:, cols], w1_scales[:, cols], mt, h, f"y{mt}{h}")
                nc.scalar.activation(rho[h][:, :, mt, :], y, ACT.Exp, scale=0.5)

        w2_grouped = sb.tile([P, N, PACK], BF16, name="w2_grouped", tag="words_then_w2", align_bytes=64)
        w2_codes = [sb.tile([P, P], U32, name=f"w2_codes{mt}", align_bytes=64) for mt in range(2)]
        w2_scales = [sb.tile([P, P], U8, name=f"w2_scales{mt}", align_bytes=64) for mt in range(2)]
        for mt in range(2):
            dst, src = interleave_views(w2_grouped[:, mt * P : (mt + 1) * P, :], w2_raw[:, :, mt * P : (mt + 1) * P])
            nc.vector.tensor_copy(dst, src)
        for mt in range(2):
            nc.vector.quantize_mx(
                out=w2_codes[mt][:].bitcast(FP8X4),
                scales=w2_scales[mt][:],
                in_=w2_grouped[:, mt * P : (mt + 1) * P, :].rearrange("p m j -> p (m j)"),
            )
        z = [[product(w2_codes[mt][:], w2_scales[mt][:], mt, h, f"z{mt}{h}") for h in range(2)] for mt in range(2)]

        dens = sb.tile([P, 2, N], F32, name="dens")
        phi = [sb.tile([P, D, N], F32, name=f"phi{mt}") for mt in range(2)]
        z_copy = [sb.tile([P, D, ATOMS], F32, name=f"z_copy{h}") for h in range(2)]
        embed = [sb.tile([P, N], F32, name=f"embed{mt}") for mt in range(2)]
        pair = [sb.tile([P, N], F32, name=f"pair{mt}") for mt in range(2)]
        energy = [sb.tile([P, N], F32, name=f"energy{mt}") for mt in range(2)]

        def atoms(h):
            return slice(h * ATOMS, (h + 1) * ATOMS)

        def add_pairs(mt):
            nc.vector.tensor_tensor(pair[mt][:], phi[mt][:, 0, :], phi[mt][:, 1, :], ALU.add)

        for h in range(2):
            nc.scalar.activation(phi[0][:, :, atoms(h)], z[0][h], ACT.Square)
        for h in range(2):
            nc.vector.tensor_tensor(dens[:, :, atoms(h)], rho[h][:, 0, :, :], rho[h][:, 1, :, :], ALU.add)
        for h in range(2):
            nc.vector.tensor_copy(z_copy[h][:], z[1][h])
        for h in range(2):
            nc.vector.tensor_tensor(phi[1][:, :, atoms(h)], z[1][h], z_copy[h][:], ALU.mult)
        for mt in range(2):
            add_pairs(mt)
        for mt in range(2):
            nc.scalar.activation(embed[mt][:], dens[:, mt, :], ACT.Sqrt, scale=2.25, bias=1.125)
            nc.vector.scalar_tensor_tensor(energy[mt][:], pair[mt][:], 0.5, embed[mt][:], ALU.mult, ALU.subtract)
            nc.sync.dma_start(out[mt * P : (mt + 1) * P, :], energy[mt][:])
